import numpy as np
import ml_dtypes


def mxq(x, axis, fmt="e4m3"):
    dtype, down = {"e4m3": (ml_dtypes.float8_e4m3fn, 7), "e5m2": (ml_dtypes.float8_e5m2, 14)}[fmt]
    v = np.moveaxis(np.asarray(x, np.float32).astype(ml_dtypes.bfloat16).astype(np.float64), axis, -1)
    blocks = v.reshape(v.shape[:-1] + (-1, 32))
    amax = np.abs(blocks).max(-1, keepdims=True)
    byte = np.maximum(np.where(amax > 0, np.frexp(amax)[1] - 1 + 127, 0) - down, 1)
    scale = np.exp2(byte - 127.0)
    codes = (blocks / scale).astype(np.float32).astype(dtype).astype(np.float64)
    return np.moveaxis((codes * scale).reshape(v.shape), -1, axis)


WIDE = False


def mx_kscale(k):
    if not WIDE:
        return np.ones(k)
    levels = np.array([10, -10, 5, -5, 0])
    if k % 512:
        return np.exp2(np.random.permutation(np.resize(levels, k // 32))).repeat(32)
    a = np.empty((k // 512, 16))
    for p in range(k // 512):
        a[p, :8] = np.random.permutation(np.resize(levels, 8))
        for g in range(8):
            far = levels[np.abs(levels - a[p, g]) >= 10]
            a[p, g + 8] = far[np.random.randint(len(far))]
    return np.exp2(a.ravel()).repeat(32)


def f64(x):
    return np.asarray(x).astype(np.float64)


def striped(idx):
    return np.tile(idx.reshape(-1, 16).T, (8, 1)).astype(np.uint16)


def unstriped(offs):
    return offs[:16].T.reshape(-1).astype(np.int64)


def striped8(idx):
    return np.concatenate([x.reshape(-1, 16).T for x in idx]).astype(np.uint16)


def runs(offs, k):
    lists = np.stack([offs[16 * r : 16 * r + 16].T.reshape(-1) for r in range(8)]).astype(np.int64)
    return lists[np.arange(k) % 512 // 64]


def pack_weight(w):
    k, n = w.shape
    w = f64(np.asarray(w, np.float32).astype(ml_dtypes.bfloat16)).reshape(k // 32, 32, n)
    amax = np.abs(w).max(1)
    byte = np.clip(np.where(amax > 0, np.frexp(amax)[1] - 1 + 127 - 7, 1), 1, 254)
    scaled = (w * np.exp2(127.0 - byte)[:, None, :]).reshape(k, n).astype(np.float32)
    words = np.ascontiguousarray(scaled.reshape(k // 512, 128, 4, n).transpose(0, 1, 3, 2)).astype(ml_dtypes.float8_e4m3fn).view(np.uint8)
    return words, np.ascontiguousarray(byte.astype(np.uint8).reshape(k // 512, 16, n))


def unpack_weight(words, scales):
    g, p, n, _ = words.shape
    vals = np.ascontiguousarray(words).view(ml_dtypes.float8_e4m3fn).astype(np.float64) * np.repeat(np.exp2(scales.astype(np.float64) - 127.0), 8, axis=1)[..., None]
    return vals.transpose(0, 1, 3, 2).reshape(g * 512, n)


def sigmoid(v):
    return 1.0 / (1.0 + np.exp(-np.maximum(v, -700.0)))


K, T, S, N, U, H = 512, 2048, 512, 512, 1024, 512


def setup_inputs():
    n = np.random.standard_normal
    s = mx_kscale(K)[:, None]
    u = mx_kscale(H)
    packed_xT = pack_weight(n((K, T)) * s)
    return {
        "x_words": packed_xT[0],
        "x_scales": packed_xT[1],
        "w1": (n((K, H)) / np.sqrt(K) / s * u).astype(np.float32),
        "w2": (n((H, N)) / np.sqrt(H) / u[:, None]).astype(np.float32),
        "pg": n((N, U)).astype(np.float32),
        "offs": striped(np.random.permutation(T)[:S]),
        "nb": striped8(np.stack([np.random.permutation(S) for _ in range(8)])),
        "slot": striped8(np.stack([np.random.permutation(U)[:S] for _ in range(8)])),
    }


def reference(x_words, x_scales, w1, w2, pg, offs, nb, slot):
    xq = unpack_weight(x_words, x_scales)[:, unstriped(offs)]
    y = mxq(f64(w1), 0, "e4m3").T @ xq
    z = y - (y[np.arange(H)[:, None], runs(nb, H)])
    h = mxq(f64(w2), 0, "e4m3").T @ mxq(z, 0, "e4m3")
    nw = h + sigmoid(h) * (f64(pg)[np.arange(N)[:, None], runs(slot, N)])
    out = f64(pg).copy()
    out[np.arange(N)[:, None], runs(slot, N)] = nw
    return out

@@ -1,0 +1,164 @@
+from contextlib import ExitStack
+
+import concourse.mybir as mybir
+
+K, T, S, N, U, H = 512, 2048, 512, 512, 1024, 512
+FLOPS = 2 * K * H * S + 2 * H * N * S
+
+F32 = mybir.dt.float32
+BF16 = mybir.dt.bfloat16
+I32 = mybir.dt.int32
+U32 = mybir.dt.uint32
+U16 = mybir.dt.uint16
+U8 = mybir.dt.uint8
+FP8X4 = mybir.dt.float8_e4m3fn_x4
+ALU = mybir.AluOpType
+ACT = mybir.ActivationFunctionType
+
+P = 128
+PACK = 4
+HALF = S // 2
+LCOLS = HALF // 16
+
+
+def tile_picked_pagefly_none_p_kernel(tc, x_words, x_scales, w1, w2, pg, offs, nb, slot, out):
+    nc = tc.nc
+    with ExitStack() as ctx:
+        keep = ctx.enter_context(tc.tile_pool(name="keep", bufs=1))
+        psum = ctx.enter_context(tc.psum_pool(name="psum", bufs=1))
+
+        def half(h):
+            return slice(h * HALF, (h + 1) * HALF)
+
+        def lhalf(h):
+            return slice(h * LCOLS, (h + 1) * LCOLS)
+
+        offs_sb = keep.tile([P, S // 16], U16, name="offs_sb")
+        nb_sb = keep.tile([P, S // 16], U16, name="nb_sb")
+        slot_sb = keep.tile([P, S // 16], U16, name="slot_sb")
+        xs = keep.tile([P, T], U8, name="xs", align_bytes=64)
+        xw = keep.tile([P, T], I32, name="xw", align_bytes=64)
+        w1_raw = [keep.tile([P, PACK, H // 2], F32, name="w1_raw%d" % h, align_bytes=64) for h in range(2)]
+
+        nc.vector.memset(xs[:].bitcast(I32), 0)
+        nc.sync.dma_start(offs_sb[:], offs)
+        for q in range(4):
+            nc.sync.dma_start(xs[32 * q : 32 * q + 4, :].bitcast(I32), x_scales[0][4 * q : 4 * q + 4, :].bitcast(I32))
+        w1_rows = w1.rearrange("(p j) c -> p j c", j=PACK)
+        w2_rows = w2.rearrange("(p j) c -> p j c", j=PACK)
+        for h in range(2):
+            nc.sync.dma_start(w1_raw[h][:], w1_rows[:, :, half(h)])
+        nc.sync.dma_start(xw[:], x_words[0].rearrange("p n r -> p (n r)").bitcast(I32))
+        nc.sync.dma_start(nb_sb[:], nb)
+        pg_rows = pg.rearrange("(p t) u -> p t u", t=PACK)
+        out_rows = out.rearrange("(p t) u -> p t u", t=PACK)
+
+        def deal_views(grouped, raw, h):
+            dst = grouped[:, :, 64 * h : 64 * (h + 1), :].rearrange("p t m j -> p m t j")
+            src = raw[:].rearrange("p j (m t) -> p m t j", t=PACK)
+            return dst, src
+
+        w1_bf = keep.tile([P, PACK, P, PACK], BF16, name="w1_bf", align_bytes=64)
+        nc.scalar.copy(*deal_views(w1_bf, w1_raw[0], 0))
+        xsq = keep.tile([P, S], U8, name="xsq", align_bytes=64)
+        nc.vector.tensor_copy(xsq[:], xs[:].indirect(offs_sb[:]))
+        nc.vector.tensor_copy(*deal_views(w1_bf, w1_raw[1], 1))
+        w1q = keep.tile([P, H], U32, name="w1q", align_bytes=64)
+        w1s = keep.tile([P, H], U8, name="w1s", align_bytes=64)
+        nc.vector.quantize_mx(out=w1q[:].bitcast(FP8X4), scales=w1s[:], in_=w1_bf[:].rearrange("p t m j -> p (t m j)"))
+        xq = [keep.tile([P, HALF], U32, name="xq%d" % h, align_bytes=64) for h in range(2)]
+        for h in range(2):
+            nc.vector.tensor_copy(xq[h][:], xw[:].bitcast(U32).indirect(offs_sb[:, lhalf(h)]))
+
+        w2_raw = [keep.tile([P, PACK, N // 2], F32, name="w2_raw%d" % h, tag="stage%d" % h, align_bytes=64) for h in range(2)]
+        for h in range(2):
+            nc.sync.dma_start(w2_raw[h][:], w2_rows[:, :, half(h)])
+        nc.sync.dma_start(slot_sb[:], slot)
+        page = [None] * PACK
+
+        def load_page(t):
+            page[t] = keep.tile([P, U], F32, name="page%d" % t, align_bytes=64)
+            nc.sync.dma_start(page[t][:], pg_rows[:, t, :])
+
+        load_page(0)
+        load_page(1)
+        load_page(2)
+        w2_bf = keep.tile([P, PACK, P, PACK], BF16, name="w2_bf", align_bytes=64)
+        nc.vector.tensor_copy(*deal_views(w2_bf, w2_raw[0], 0))
+
+        load_page(3)
+        wins = []
+        zneg_all = keep.tile([P, 2, PACK, HALF], F32, name="zneg", tag="stage0", align_bytes=64)
+        zneg = [zneg_all[:, h] for h in range(2)]
+        for t in range(PACK):
+            rows = slice(t * P, (t + 1) * P)
+            win = keep.tile([P, S], F32, name="win%d" % t, align_bytes=64)
+            wins.append(win)
+            own = [keep.tile([P, HALF], F32, name="own%d_%d" % (t, h), align_bytes=64) for h in range(2)]
+            for h in range(2):
+                acc = psum.tile([P, HALF], F32, name="y%d_%d" % (t, h), tag="bank%d" % (2 * (t % 2) + h))
+                nc.tensor.matmul_mx(out=acc[:], lhsT=w1q[:, rows].bitcast(FP8X4), lhsT_scale=w1s[:, rows],
+                                    rhs=xq[h][:].bitcast(FP8X4), rhs_scale=xsq[:, half(h)], start=True, stop=True)
+                nc.scalar.copy(win[:, half(h)], acc[:])
+                nc.scalar.copy(own[h][:], acc[:])
+            for h in range(2):
+                nc.vector.tensor_tensor(zneg[h][:, t, :], win[:].indirect(nb_sb[:, lhalf(h)]), own[h][:], ALU.subtract)
+
+        nc.scalar.copy(*deal_views(w2_bf, w2_raw[1], 1))
+        z_bf = [keep.tile([P, HALF, PACK], BF16, name="z_bf%d" % h, align_bytes=64) for h in range(2)]
+        zq = keep.tile([P, S], U32, name="zq", align_bytes=64)
+        zs = keep.tile([P, S], U8, name="zs", align_bytes=64)
+        w2q = keep.tile([P, N], U32, name="w2q", align_bytes=64)
+        w2s = keep.tile([P, N], U8, name="w2s", align_bytes=64)
+
+        def weave(h):
+            nc.vector.tensor_scalar(z_bf[h][:].rearrange("p (c i) t -> p c t i", i=4),
+                                    zneg[h].rearrange("p t (c i) -> p c t i", i=4), -1.0, None, ALU.mult)
+
+        def quant_z(h):
+            nc.vector.quantize_mx(out=zq[:, half(h)].bitcast(FP8X4), scales=zs[:, half(h)], in_=z_bf[h][:].rearrange("p c t -> p (c t)"))
+
+        def quant_w2(h):
+            nc.vector.quantize_mx(out=w2q[:, half(h)].bitcast(FP8X4), scales=w2s[:, half(h)],
+                                  in_=w2_bf[:, 2 * h : 2 * h + 2].rearrange("p t m j -> p (t m j)"))
+
+        weave(0)
+        quant_w2(0)
+        quant_z(0)
+        weave(1)
+        quant_w2(1)
+        quant_z(1)
+
+        hid = [keep.tile([P, S], F32, name="hid%d" % t, align_bytes=64) for t in range(PACK)]
+        gate = [keep.tile([P, S], F32, name="gate%d" % t, align_bytes=64) for t in range(PACK)]
+        kept = [keep.tile([P, S], F32, name="kept%d" % t, align_bytes=64) for t in range(PACK)]
+        pieces = [[(half(0), lhalf(0)), (half(1), lhalf(1))]] * 2 + [[(slice(0, S), slice(0, S // 16))]] * 2
+        banks = {(0, 0): 4, (1, 0): 5, (0, 1): 6, (1, 1): 7, (2, 0): 0, (3, 0): 1}
+        accs = {}
+
+        def second(t, i):
+            cols, lcols = pieces[t][i]
+            rows = slice(t * P, (t + 1) * P)
+            acc = psum.tile([P, cols.stop - cols.start], F32, name="h%d_%d" % (t, i), tag="bank%d" % banks[t, i])
+            accs[t, i] = acc
+            nc.tensor.matmul_mx(out=acc[:], lhsT=w2q[:, rows].bitcast(FP8X4), lhsT_scale=w2s[:, rows],
+                                rhs=zq[:, cols].bitcast(FP8X4), rhs_scale=zs[:, cols], start=True, stop=True)
+            nc.scalar.activation(gate[t][:, cols], acc[:], ACT.Sigmoid)
+            nc.vector.tensor_tensor(kept[t][:, cols], page[t][:].indirect(slot_sb[:, lcols]), gate[t][:, cols], ALU.mult)
+
+        def put(t):
+            for i, (cols, lcols) in enumerate(pieces[t]):
+                nc.scalar.copy(hid[t][:, cols], accs[t, i][:])
+            nc.vector.tensor_tensor(page[t][:].indirect(slot_sb[:]), kept[t][:], hid[t][:], ALU.add)
+            nc.sync.dma_start(out_rows[:, t, :], page[t][:])
+
+        second(0, 0)
+        second(1, 0)
+        second(0, 1)
+        second(1, 1)
+        put(0)
+        second(2, 0)
+        put(1)
+        second(3, 0)
+        put(2)
+        put(3)

@@ -83,7 +83,7 @@ def tile_picked_pagefly_none_p_kernel(tc, x_words, x_scales, w1, w2, pg, offs, n
         load_page(0)
         load_page(1)
         load_page(2)
-        w2_bf = keep.tile([P, PACK, P, PACK], BF16, name="w2_bf", align_bytes=64)
+        w2_bf = keep.tile([P, PACK, P, PACK], BF16, name="w2_bf", tag="w2_bf", align_bytes=64)
         nc.vector.tensor_copy(*deal_views(w2_bf, w2_raw[0], 0))
 
         load_page(3)
@@ -92,7 +92,7 @@ def tile_picked_pagefly_none_p_kernel(tc, x_words, x_scales, w1, w2, pg, offs, n
         zneg = [zneg_all[:, h] for h in range(2)]
         for t in range(PACK):
             rows = slice(t * P, (t + 1) * P)
-            win = keep.tile([P, S], F32, name="win%d" % t, align_bytes=64)
+            win = keep.tile([P, S], F32, name="win%d" % t, tag="win%d" % t, align_bytes=64)
             wins.append(win)
             own = [keep.tile([P, HALF], F32, name="own%d_%d" % (t, h), align_bytes=64) for h in range(2)]
             for h in range(2):
@@ -105,7 +105,7 @@ def tile_picked_pagefly_none_p_kernel(tc, x_words, x_scales, w1, w2, pg, offs, n
                 nc.vector.tensor_tensor(zneg[h][:, t, :], win[:].indirect(nb_sb[:, lhalf(h)]), own[h][:], ALU.subtract)
 
         nc.scalar.copy(*deal_views(w2_bf, w2_raw[1], 1))
-        z_bf = [keep.tile([P, HALF, PACK], BF16, name="z_bf%d" % h, align_bytes=64) for h in range(2)]
+        z_bf = [keep.tile([P, HALF, PACK], BF16, name="z_bf%d" % h, tag="z_bf%d" % h, align_bytes=64) for h in range(2)]
         zq = keep.tile([P, S], U32, name="zq", align_bytes=64)
         zs = keep.tile([P, S], U8, name="zs", align_bytes=64)
         w2q = keep.tile([P, N], U32, name="w2q", align_bytes=64)
@@ -122,43 +122,36 @@ def tile_picked_pagefly_none_p_kernel(tc, x_words, x_scales, w1, w2, pg, offs, n
             nc.vector.quantize_mx(out=w2q[:, half(h)].bitcast(FP8X4), scales=w2s[:, half(h)],
                                   in_=w2_bf[:, 2 * h : 2 * h + 2].rearrange("p t m j -> p (t m j)"))
 
+        old = [None] * PACK
+
+        def fetch(t, tag):
+            old[t] = keep.tile([P, S], F32, name="old%d" % t, tag=tag, align_bytes=64)
+            nc.vector.tensor_copy(old[t][:], page[t][:].indirect(slot_sb[:]))
+
         weave(0)
         quant_w2(0)
         quant_z(0)
         weave(1)
-        quant_w2(1)
+        fetch(0, "win3")
         quant_z(1)
+        quant_w2(1)
+        fetch(1, "z_bf0")
+        fetch(2, "z_bf1")
+        fetch(3, "w2_bf")
 
-        hid = [keep.tile([P, S], F32, name="hid%d" % t, align_bytes=64) for t in range(PACK)]
-        gate = [keep.tile([P, S], F32, name="gate%d" % t, align_bytes=64) for t in range(PACK)]
-        kept = [keep.tile([P, S], F32, name="kept%d" % t, align_bytes=64) for t in range(PACK)]
-        pieces = [[(half(0), lhalf(0)), (half(1), lhalf(1))]] * 2 + [[(slice(0, S), slice(0, S // 16))]] * 2
-        banks = {(0, 0): 4, (1, 0): 5, (0, 1): 6, (1, 1): 7, (2, 0): 0, (3, 0): 1}
-        accs = {}
-
-        def second(t, i):
-            cols, lcols = pieces[t][i]
+        for t in range(PACK):
             rows = slice(t * P, (t + 1) * P)
-            acc = psum.tile([P, cols.stop - cols.start], F32, name="h%d_%d" % (t, i), tag="bank%d" % banks[t, i])
-            accs[t, i] = acc
-            nc.tensor.matmul_mx(out=acc[:], lhsT=w2q[:, rows].bitcast(FP8X4), lhsT_scale=w2s[:, rows],
-                                rhs=zq[:, cols].bitcast(FP8X4), rhs_scale=zs[:, cols], start=True, stop=True)
-            nc.scalar.activation(gate[t][:, cols], acc[:], ACT.Sigmoid)
-            nc.vector.tensor_tensor(kept[t][:, cols], page[t][:].indirect(slot_sb[:, lcols]), gate[t][:, cols], ALU.mult)
-
-        def put(t):
-            for i, (cols, lcols) in enumerate(pieces[t]):
-                nc.scalar.copy(hid[t][:, cols], accs[t, i][:])
-            nc.vector.tensor_tensor(page[t][:].indirect(slot_sb[:]), kept[t][:], hid[t][:], ALU.add)
+            hid = keep.tile([P, S], F32, name="hid%d" % t, align_bytes=64)
+            gate = keep.tile([P, S], F32, name="gate%d" % t, align_bytes=64)
+            kept = keep.tile([P, S], F32, name="kept%d" % t, align_bytes=64)
+            new = keep.tile([P, S], F32, name="new%d" % t, align_bytes=64)
+            for i, cols in enumerate([half(0), half(1)] if t == 0 else [slice(0, S)]):
+                acc = psum.tile([P, cols.stop - cols.start], F32, name="h%d_%d" % (t, i), tag="bank%d" % ((4 + t + i + min(t, 1)) % 8))
+                nc.tensor.matmul_mx(out=acc[:], lhsT=w2q[:, rows].bitcast(FP8X4), lhsT_scale=w2s[:, rows],
+                                    rhs=zq[:, cols].bitcast(FP8X4), rhs_scale=zs[:, cols], start=True, stop=True)
+                nc.scalar.activation(gate[:, cols], acc[:], ACT.Sigmoid)
+                nc.scalar.copy(hid[:, cols], acc[:])
+                nc.gpsimd.tensor_tensor(kept[:, cols], old[t][:, cols], gate[:, cols], ALU.mult)
+                nc.gpsimd.tensor_tensor(new[:, cols], kept[:, cols], hid[:, cols], ALU.add)
+            nc.vector.tensor_copy(page[t][:].indirect(slot_sb[:]), new[:])
             nc.sync.dma_start(out_rows[:, t, :], page[t][:])
-
-        second(0, 0)
-        second(1, 0)
-        second(0, 1)
-        second(1, 1)
-        put(0)
-        second(2, 0)
-        put(1)
-        second(3, 0)
-        put(2)
-        put(3)

from contextlib import ExitStack

import concourse.mybir as mybir

K, T, S, N, U, H = 512, 2048, 512, 512, 1024, 512
FLOPS = 2 * K * H * S + 2 * H * N * S

F32 = mybir.dt.float32
BF16 = mybir.dt.bfloat16
I32 = mybir.dt.int32
U32 = mybir.dt.uint32
U16 = mybir.dt.uint16
U8 = mybir.dt.uint8
FP8X4 = mybir.dt.float8_e4m3fn_x4
ALU = mybir.AluOpType
ACT = mybir.ActivationFunctionType

P = 128
PACK = 4
HALF = S // 2
LCOLS = HALF // 16


def tile_picked_pagefly_none_p_kernel(tc, x_words, x_scales, w1, w2, pg, offs, nb, slot, out):
    nc = tc.nc
    with ExitStack() as ctx:
        keep = ctx.enter_context(tc.tile_pool(name="keep", bufs=1))
        psum = ctx.enter_context(tc.psum_pool(name="psum", bufs=1))

        def half(h):
            return slice(h * HALF, (h + 1) * HALF)

        def lhalf(h):
            return slice(h * LCOLS, (h + 1) * LCOLS)

        offs_sb = keep.tile([P, S // 16], U16, name="offs_sb")
        nb_sb = keep.tile([P, S // 16], U16, name="nb_sb")
        slot_sb = keep.tile([P, S // 16], U16, name="slot_sb")
        xs = keep.tile([P, T], U8, name="xs", align_bytes=64)
        xw = keep.tile([P, T], I32, name="xw", align_bytes=64)
        w1_raw = [keep.tile([P, PACK, H // 2], F32, name="w1_raw%d" % h, align_bytes=64) for h in range(2)]

        nc.vector.memset(xs[:].bitcast(I32), 0)
        nc.sync.dma_start(offs_sb[:], offs)
        for q in range(4):
            nc.sync.dma_start(xs[32 * q : 32 * q + 4, :].bitcast(I32), x_scales[0][4 * q : 4 * q + 4, :].bitcast(I32))
        w1_rows = w1.rearrange("(p j) c -> p j c", j=PACK)
        w2_rows = w2.rearrange("(p j) c -> p j c", j=PACK)
        for h in range(2):
            nc.sync.dma_start(w1_raw[h][:], w1_rows[:, :, half(h)])
        nc.sync.dma_start(xw[:], x_words[0].rearrange("p n r -> p (n r)").bitcast(I32))
        nc.sync.dma_start(nb_sb[:], nb)
        pg_rows = pg.rearrange("(p t) u -> p t u", t=PACK)
        out_rows = out.rearrange("(p t) u -> p t u", t=PACK)

        def deal_views(grouped, raw, h):
            dst = grouped[:, :, 64 * h : 64 * (h + 1), :].rearrange("p t m j -> p m t j")
            src = raw[:].rearrange("p j (m t) -> p m t j", t=PACK)
            return dst, src

        w1_bf = keep.tile([P, PACK, P, PACK], BF16, name="w1_bf", align_bytes=64)
        nc.scalar.copy(*deal_views(w1_bf, w1_raw[0], 0))
        xsq = keep.tile([P, S], U8, name="xsq", align_bytes=64)
        nc.vector.tensor_copy(xsq[:], xs[:].indirect(offs_sb[:]))
        nc.vector.tensor_copy(*deal_views(w1_bf, w1_raw[1], 1))
        w1q = keep.tile([P, H], U32, name="w1q", align_bytes=64)
        w1s = keep.tile([P, H], U8, name="w1s", align_bytes=64)
        nc.vector.quantize_mx(out=w1q[:].bitcast(FP8X4), scales=w1s[:], in_=w1_bf[:].rearrange("p t m j -> p (t m j)"))
        xq = [keep.tile([P, HALF], U32, name="xq%d" % h, align_bytes=64) for h in range(2)]
        for h in range(2):
            nc.vector.tensor_copy(xq[h][:], xw[:].bitcast(U32).indirect(offs_sb[:, lhalf(h)]))

        w2_raw = [keep.tile([P, PACK, N // 2], F32, name="w2_raw%d" % h, tag="stage%d" % h, align_bytes=64) for h in range(2)]
        for h in range(2):
            nc.sync.dma_start(w2_raw[h][:], w2_rows[:, :, half(h)])
        nc.sync.dma_start(slot_sb[:], slot)
        page = [None] * PACK

        def load_page(t):
            page[t] = keep.tile([P, U], F32, name="page%d" % t, align_bytes=64)
            nc.sync.dma_start(page[t][:], pg_rows[:, t, :])

        load_page(0)
        load_page(1)
        load_page(2)
        w2_bf = keep.tile([P, PACK, P, PACK], BF16, name="w2_bf", tag="w2_bf", align_bytes=64)
        nc.vector.tensor_copy(*deal_views(w2_bf, w2_raw[0], 0))

        load_page(3)
        wins = []
        zneg_all = keep.tile([P, 2, PACK, HALF], F32, name="zneg", tag="stage0", align_bytes=64)
        zneg = [zneg_all[:, h] for h in range(2)]
        for t in range(PACK):
            rows = slice(t * P, (t + 1) * P)
            win = keep.tile([P, S], F32, name="win%d" % t, tag="win%d" % t, align_bytes=64)
            wins.append(win)
            own = [keep.tile([P, HALF], F32, name="own%d_%d" % (t, h), align_bytes=64) for h in range(2)]
            for h in range(2):
                acc = psum.tile([P, HALF], F32, name="y%d_%d" % (t, h), tag="bank%d" % (2 * (t % 2) + h))
                nc.tensor.matmul_mx(out=acc[:], lhsT=w1q[:, rows].bitcast(FP8X4), lhsT_scale=w1s[:, rows],
                                    rhs=xq[h][:].bitcast(FP8X4), rhs_scale=xsq[:, half(h)], start=True, stop=True)
                nc.scalar.copy(win[:, half(h)], acc[:])
                nc.scalar.copy(own[h][:], acc[:])
            for h in range(2):
                nc.vector.tensor_tensor(zneg[h][:, t, :], win[:].indirect(nb_sb[:, lhalf(h)]), own[h][:], ALU.subtract)

        nc.scalar.copy(*deal_views(w2_bf, w2_raw[1], 1))
        z_bf = [keep.tile([P, HALF, PACK], BF16, name="z_bf%d" % h, tag="z_bf%d" % h, align_bytes=64) for h in range(2)]
        zq = keep.tile([P, S], U32, name="zq", align_bytes=64)
        zs = keep.tile([P, S], U8, name="zs", align_bytes=64)
        w2q = keep.tile([P, N], U32, name="w2q", align_bytes=64)
        w2s = keep.tile([P, N], U8, name="w2s", align_bytes=64)

        def weave(h):
            nc.vector.tensor_scalar(z_bf[h][:].rearrange("p (c i) t -> p c t i", i=4),
                                    zneg[h].rearrange("p t (c i) -> p c t i", i=4), -1.0, None, ALU.mult)

        def quant_z(h):
            nc.vector.quantize_mx(out=zq[:, half(h)].bitcast(FP8X4), scales=zs[:, half(h)], in_=z_bf[h][:].rearrange("p c t -> p (c t)"))

        def quant_w2(h):
            nc.vector.quantize_mx(out=w2q[:, half(h)].bitcast(FP8X4), scales=w2s[:, half(h)],
                                  in_=w2_bf[:, 2 * h : 2 * h + 2].rearrange("p t m j -> p (t m j)"))

        old = [None] * PACK

        def fetch(t, tag):
            old[t] = keep.tile([P, S], F32, name="old%d" % t, tag=tag, align_bytes=64)
            nc.vector.tensor_copy(old[t][:], page[t][:].indirect(slot_sb[:]))

        weave(0)
        quant_w2(0)
        quant_z(0)
        weave(1)
        fetch(0, "win3")
        quant_z(1)
        quant_w2(1)
        fetch(1, "z_bf0")
        fetch(2, "z_bf1")
        fetch(3, "w2_bf")

        for t in range(PACK):
            rows = slice(t * P, (t + 1) * P)
            hid = keep.tile([P, S], F32, name="hid%d" % t, align_bytes=64)
            gate = keep.tile([P, S], F32, name="gate%d" % t, align_bytes=64)
            kept = keep.tile([P, S], F32, name="kept%d" % t, align_bytes=64)
            new = keep.tile([P, S], F32, name="new%d" % t, align_bytes=64)
            for i, cols in enumerate([half(0), half(1)] if t == 0 else [slice(0, S)]):
                acc = psum.tile([P, cols.stop - cols.start], F32, name="h%d_%d" % (t, i), tag="bank%d" % ((4 + t + i + min(t, 1)) % 8))
                nc.tensor.matmul_mx(out=acc[:], lhsT=w2q[:, rows].bitcast(FP8X4), lhsT_scale=w2s[:, rows],
                                    rhs=zq[:, cols].bitcast(FP8X4), rhs_scale=zs[:, cols], start=True, stop=True)
                nc.scalar.activation(gate[:, cols], acc[:], ACT.Sigmoid)
                nc.scalar.copy(hid[:, cols], acc[:])
                nc.gpsimd.tensor_tensor(kept[:, cols], old[t][:, cols], gate[:, cols], ALU.mult)
                nc.gpsimd.tensor_tensor(new[:, cols], kept[:, cols], hid[:, cols], ALU.add)
            nc.vector.tensor_copy(page[t][:].indirect(slot_sb[:]), new[:])
            nc.sync.dma_start(out_rows[:, t, :], page[t][:])
